import numpy as np
import ml_dtypes


def mxq(x, axis, fmt="e4m3"):
    dtype, down = {"e4m3": (ml_dtypes.float8_e4m3fn, 7), "e5m2": (ml_dtypes.float8_e5m2, 14)}[fmt]
    v = np.moveaxis(np.asarray(x, np.float32).astype(ml_dtypes.bfloat16).astype(np.float64), axis, -1)
    blocks = v.reshape(v.shape[:-1] + (-1, 32))
    amax = np.abs(blocks).max(-1, keepdims=True)
    byte = np.maximum(np.where(amax > 0, np.frexp(amax)[1] - 1 + 127, 0) - down, 1)
    scale = np.exp2(byte - 127.0)
    codes = (blocks / scale).astype(np.float32).astype(dtype).astype(np.float64)
    return np.moveaxis((codes * scale).reshape(v.shape), -1, axis)


WIDE = False


def mx_kscale(k):
    if not WIDE:
        return np.ones(k)
    levels = np.array([10, -10, 5, -5, 0])
    if k % 512:
        return np.exp2(np.random.permutation(np.resize(levels, k // 32))).repeat(32)
    a = np.empty((k // 512, 16))
    for p in range(k // 512):
        a[p, :8] = np.random.permutation(np.resize(levels, 8))
        for g in range(8):
            far = levels[np.abs(levels - a[p, g]) >= 10]
            a[p, g + 8] = far[np.random.randint(len(far))]
    return np.exp2(a.ravel()).repeat(32)


def f64(x):
    return np.asarray(x).astype(np.float64)


def striped(idx):
    return np.tile(idx.reshape(-1, 16).T, (8, 1)).astype(np.uint16)


def unstriped(offs):
    return offs[:16].T.reshape(-1).astype(np.int64)


def striped8(idx):
    return np.concatenate([x.reshape(-1, 16).T for x in idx]).astype(np.uint16)


def runs(offs, k):
    lists = np.stack([offs[16 * r : 16 * r + 16].T.reshape(-1) for r in range(8)]).astype(np.int64)
    return lists[np.arange(k) % 512 // 64]


def pack_weight(w):
    k, n = w.shape
    w = f64(np.asarray(w, np.float32).astype(ml_dtypes.bfloat16)).reshape(k // 32, 32, n)
    amax = np.abs(w).max(1)
    byte = np.clip(np.where(amax > 0, np.frexp(amax)[1] - 1 + 127 - 7, 1), 1, 254)
    scaled = (w * np.exp2(127.0 - byte)[:, None, :]).reshape(k, n).astype(np.float32)
    words = np.ascontiguousarray(scaled.reshape(k // 512, 128, 4, n).transpose(0, 1, 3, 2)).astype(ml_dtypes.float8_e4m3fn).view(np.uint8)
    return words, np.ascontiguousarray(byte.astype(np.uint8).reshape(k // 512, 16, n))


def unpack_weight(words, scales):
    g, p, n, _ = words.shape
    vals = np.ascontiguousarray(words).view(ml_dtypes.float8_e4m3fn).astype(np.float64) * np.repeat(np.exp2(scales.astype(np.float64) - 127.0), 8, axis=1)[..., None]
    return vals.transpose(0, 1, 3, 2).reshape(g * 512, n)


K, T, S, G, H, W = 512, 1024, 512, 2048, 512, 256


def setup_inputs():
    n = np.random.standard_normal
    s = mx_kscale(K)[:, None]
    packed_xT = pack_weight(n((K, T)) * s)
    packed_dT = pack_weight(n((K, G)) / s)
    perm = np.stack([np.random.permutation(S) for _ in range(8)])
    perm2 = np.stack([np.random.permutation(S) for _ in range(8)])
    perm3 = np.random.permutation(S)
    perm4 = np.random.permutation(S)
    return {
        "x_words": packed_xT[0],
        "x_scales": packed_xT[1],
        "d_words": packed_dT[0],
        "d_scales": packed_dT[1],
        "gs": (np.random.uniform(0.5, 1.5, (K, 1)) * s).astype(np.float32),
        "offs": striped(np.random.permutation(T)[:S]),
        "k1": striped8(np.random.randint(0, G, (8, H))),
        "two": striped(np.random.permutation(T)[:S]),
        "k2": striped8(np.random.randint(0, G, (8, H))),
        "hz": striped8(np.random.randint(0, T, (8, S))),
        "k3": striped8(np.random.randint(0, G, (8, H))),
        "n1": striped8(perm[:, :W]),
        "n2": striped8(perm[:, W:]),
        "n3": striped8(perm2[:, :W]),
        "n4": striped8(perm2[:, W:]),
        "n5": striped8(np.stack([np.random.permutation(S) for _ in range(8)])),
        "k4": striped8(np.random.randint(0, G, (8, H))),
        "k5": striped8(np.random.randint(0, G, (8, H))),
        "duo": striped(np.random.permutation(T)[:S]),
        "n6": striped(perm3[:W]),
        "n7": striped(perm3[W:]),
        "n8": striped(perm4[:W]),
        "n9": striped(perm4[W:]),
    }


def reference(x_words, x_scales, d_words, d_scales, gs, offs, k1, two, k2, hz, k3, n1, n2, n3, n4, n5, k4, k5, duo, n6, n7, n8, n9):
    d_k4 = unpack_weight(d_words, d_scales)[np.arange(K)[:, None], runs(k4, K)]
    d_k1 = unpack_weight(d_words, d_scales)[np.arange(K)[:, None], runs(k1, K)]
    xq = unpack_weight(x_words, x_scales)[:, unstriped(offs)]
    d_k2 = unpack_weight(d_words, d_scales)[np.arange(K)[:, None], runs(k2, K)]
    x_two = unpack_weight(x_words, x_scales)[:, unstriped(two)]
    d_k3 = unpack_weight(d_words, d_scales)[np.arange(K)[:, None], runs(k3, K)]
    x_hz = unpack_weight(x_words, x_scales)[np.arange(K)[:, None], runs(hz, K)]
    h = 0.0625 * (d_k1.T @ xq + d_k2.T @ x_two + d_k3.T @ x_hz)
    pa = h[np.arange(H)[:, None], runs(n1, H)]
    pb = h[np.arange(H)[:, None], runs(n2, H)]
    rb = pa + pb
    ra = np.minimum(pa, pb)
    ua = np.zeros((H, S))
    ua[np.arange(H)[:, None], runs(n3, H)] = ra
    ub = ua.copy()
    ub[np.arange(H)[:, None], runs(n4, H)] = rb
    ds = np.zeros((H, S))
    ds[np.arange(H)[:, None], runs(n5, H)] = ub
    z = f64(gs) * (ub - ds)
    d_k5 = unpack_weight(d_words, d_scales)[np.arange(K)[:, None], runs(k5, K)]
    x_duo = unpack_weight(x_words, x_scales)[:, unstriped(duo)]
    h2 = 0.0625 * ((d_k4.T @ mxq(z, 0, "e4m3") + d_k5.T @ x_duo))
    pa2 = h2[:, unstriped(n6)]
    pb2 = h2[:, unstriped(n7)]
    rb2 = pa2 - pb2
    ra2 = np.maximum(pa2, pb2)
    ua2 = np.zeros((H, S))
    ua2[:, unstriped(n8)] = ra2
    out = ua2.copy()
    out[:, unstriped(n9)] = rb2
    return out

@@ -1,0 +1,226 @@
+from contextlib import ExitStack
+
+import concourse.mybir as mybir
+
+F32 = mybir.dt.float32
+BF16 = mybir.dt.bfloat16
+I32 = mybir.dt.int32
+U32 = mybir.dt.uint32
+U16 = mybir.dt.uint16
+U8 = mybir.dt.uint8
+FP8X4 = mybir.dt.float8_e4m3fn_x4
+ALU = mybir.AluOpType
+COPY = mybir.ActivationFunctionType.Copy
+
+P = 128
+S = 512
+W = 256
+T = 1024
+G = 2048
+FLOPS = 5 * 2 * 512 * 512 * 512
+
+
+def tile_picked_mtthzmtcpsdcpmx_none_p_kernel(
+    tc, x_words, x_scales, d_words, d_scales, gs, offs, k1, two, k2, hz, k3, n1, n2, n3, n4, n5, k4, k5, duo, n6, n7, n8, n9, out
+):
+    nc = tc.nc
+    with ExitStack() as ctx:
+        keep = ctx.enter_context(tc.tile_pool(name="keep", bufs=1))
+        reuse = ctx.enter_context(tc.tile_pool(name="reuse", bufs=1))
+        psum = ctx.enter_context(tc.psum_pool(name="psum", bufs=1))
+
+        def new(name, cols, dtype):
+            return keep.tile([P, cols], dtype, name=name, align_bytes=64)
+
+        def placed(name, cols, dtype, offset):
+            return reuse.tile([P, cols], dtype, name=name, align_bytes=64, offset=offset)
+
+        x_bytes = new("x_bytes", T, U8)
+        d_bytes = new("d_bytes", G, U8)
+        x_table = new("x_table", T, U32)
+        d_table = new("d_table", G, U32)
+        for tile_, src, cols in ((d_bytes, d_scales, G), (x_bytes, x_scales, T)):
+            rows = src[0].bitcast(I32)
+            nc.scalar.dma_start(out=tile_[:].bitcast(I32), in_=rows.unsqueeze(1).to_broadcast([16, 8, cols // 4]))
+        for tile_, src in ((d_table, d_words), (x_table, x_words)):
+            nc.scalar.dma_start(out=tile_[:].bitcast(I32), in_=src[0].rearrange("p n t -> p (n t)").bitcast(I32))
+
+        lists = {}
+
+        def load_lists(*named):
+            for name, src in named:
+                lists[name] = keep.tile([P, src.shape[1]], U16, name="list_" + name)
+                nc.sync.dma_start(lists[name][:], src)
+
+        load_lists(("k1", k1), ("k2", k2), ("k3", k3), ("offs", offs), ("two", two), ("hz", hz))
+
+        def whole(name):
+            return lists[name][:]
+
+        def half(name, h):
+            return lists[name][:, 16 * h : 16 * (h + 1)]
+
+        def gather(dst, table, offsets):
+            nc.vector.tensor_copy(dst, table[:].indirect(offsets))
+
+        def place_rows(queue, plane, first, gathered):
+            for q in range(0, P, 32):
+                queue.dma_start(out=plane[q + first : q + first + 4, :].bitcast(I32), in_=gathered[q : q + 32 : 8, :].bitcast(I32))
+
+        x_planes = new("x_planes", 3 * S, U8)
+        k_packed = placed("k_packed", S, U8, 14336 + 6144)
+        early_planes = new("early_planes", S + 2 * W, U8)
+        late_planes = new("late_planes", 2 * W, U8)
+        for plane in (x_planes, k_packed, early_planes, late_planes):
+            nc.vector.memset(plane[:].bitcast(I32), 0)
+
+        x_names = ("offs", "two", "hz")
+        k_names = ("k1", "k2", "k3")
+        for a, name in enumerate(k_names):
+            k_got = new("k_got%d" % a, S, U8)
+            gather(k_got[:], d_bytes, whole(name))
+            place_rows(nc.sync, k_packed, 4 * a, k_got)
+        x_got = new("x_got", 3 * S, U8)
+        for a, name in enumerate(x_names):
+            gather(x_got[:, a * S : (a + 1) * S], x_bytes, whole(name))
+        place_rows(nc.scalar, x_planes, 0, x_got)
+
+        load_lists(("duo", duo), ("k4", k4), ("k5", k5), ("n1", n1), ("n2", n2), ("n4", n4), ("n3", n3), ("n5", n5))
+        gain = new("gain", 4, F32)
+        nc.sync.dma_start(out=gain[:], in_=gs.rearrange("(p t) o -> p (t o)", t=4))
+        load_lists(("n6", n6), ("n7", n7), ("n9", n9), ("n8", n8))
+
+        raw = placed("raw", 3 * S, U32, 14336)
+        k_codes = new("k_codes", 3 * S, U32)
+        x_codes = [new("x_codes0", S, U32), placed("x_codes1", S, U32, 14336 + 4352), placed("x_codes2", S, U32, 14336 + 6400)]
+        k_planes = new("k_planes", S, U8)
+
+        def deal(dst, src, run):
+            nc.vector.tensor_copy(
+                dst[:].rearrange("p (t c i) -> p c t i", t=4, i=run),
+                src[:].rearrange("p (c i t) -> p c t i", t=4, i=run),
+            )
+
+        for a, name in enumerate(k_names):
+            gather(raw[:, a * S : (a + 1) * S], d_table, whole(name))
+        deal(k_planes, k_packed, 16)
+        gather(x_codes[0][:], x_table, whole("offs"))
+        deal(k_codes, raw, 4)
+        gather(x_codes[1][:], x_table, whole("two"))
+        gather(x_codes[2][:], x_table, whole("hz"))
+
+        h_banks = [psum.tile([P, S], F32, name="h_bank%d" % t) for t in range(4)]
+        for t in range(4):
+            cols = slice(t * P, (t + 1) * P)
+            for a in range(3):
+                nc.tensor.matmul_mx(
+                    out=h_banks[t][:],
+                    lhsT=k_codes[:, (3 * t + a) * P : (3 * t + a + 1) * P].bitcast(FP8X4),
+                    lhsT_scale=k_planes[4 * a : P, cols],
+                    rhs=x_codes[a][:].bitcast(FP8X4),
+                    rhs_scale=x_planes[:, a * S : (a + 1) * S],
+                    start=(a == 0),
+                    stop=(a == 2),
+                )
+
+        pa, pb = [], []
+        for t in range(4):
+            h = keep.tile([P, S], F32, name="h%d" % t, tag="window", align_bytes=64)
+            nc.scalar.activation(h[:], h_banks[t][:], COPY, scale=0.0625)
+            pa.append(new("pa%d" % t, W, F32))
+            pb.append(new("pb%d" % t, W, F32))
+            nc.scalar.activation(pa[t][:], h[:].indirect(whole("n1")), COPY)
+            nc.scalar.activation(pb[t][:], h[:].indirect(whole("n2")), COPY)
+
+        ub = [new("ub%d" % t, S, F32) for t in range(3)] + [placed("ub3", S, F32, 2048)]
+        ds = [new("ds%d" % t, 2 * S, F32) for t in range(3)] + [placed("ds3", 2 * S, F32, 4096)]
+        diff = [new("diff%d" % t, S, F32) for t in range(3)] + [placed("diff3", S, F32, 12288)]
+        z = placed("z", 4 * S, BF16, 8192)
+        z_by_slot = z[:].rearrange("p (j t) -> p j t", t=4)
+
+        def send(t):
+            nc.vector.tensor_copy(ds[t][:].indirect(whole("n5")), ub[t][:])
+
+        def finish(t):
+            nc.vector.tensor_tensor(diff[t][:], ub[t][:], ds[t][:, 0:S], ALU.subtract)
+            nc.scalar.activation(z_by_slot[:, :, t], diff[t][:], COPY, scale=gain[:, t : t + 1])
+
+        for t in range(4):
+            ra = new("ra%d" % t, W, F32)
+            nc.vector.tensor_tensor(ra[:], pa[t][:], pb[t][:], ALU.min)
+            nc.vector.tensor_tensor(ub[t][:].indirect(whole("n4")), pa[t][:], pb[t][:], ALU.add)
+            if t > 0:
+                send(t - 1)
+            nc.vector.tensor_copy(ub[t][:].indirect(whole("n3")), ra[:])
+            if t > 0:
+                finish(t - 1)
+        send(3)
+        finish(3)
+        z_codes = new("z_codes", S, U32)
+        z_plane = new("z_plane", S, U8)
+        nc.vector.quantize_mx(out=z_codes[:].bitcast(FP8X4), scales=z_plane[:], in_=z[:])
+
+        early_got = placed("early_got", S + 2 * W, U8, 14336)
+        gather(early_got[:, 0:S], x_bytes, whole("duo"))
+        gather(early_got[:, S : S + W], d_bytes, half("k4", 0))
+        gather(early_got[:, S + W : S + 2 * W], d_bytes, half("k5", 0))
+        place_rows(nc.sync, early_planes, 0, early_got)
+        k4_early = placed("k4_early", W, U32, 14336 + 1024)
+        gather(k4_early[:], d_table, half("k4", 0))
+        duo_codes = placed("duo_codes", S, U32, 2048)
+        gather(duo_codes[:], x_table, whole("duo"))
+        k5_early = placed("k5_early", W, U32, 4096)
+        gather(k5_early[:], d_table, half("k5", 0))
+        late_got = placed("late_got", 2 * W, U8, 12288)
+        gather(late_got[:, 0:W], d_bytes, half("k4", 1))
+        gather(late_got[:, W : 2 * W], d_bytes, half("k5", 1))
+        place_rows(nc.sync, late_planes, 0, late_got)
+        late_codes = placed("late_codes", 2 * W, U32, 8192)
+        gather(late_codes[:, 0:W], d_table, half("k4", 1))
+        gather(late_codes[:, W : 2 * W], d_table, half("k5", 1))
+
+        pa2, nb2 = [], []
+        for m in range(4):
+            c = (m % 2) * P
+            if m < 2:
+                k4_op = (k4_early[:, c : c + P], early_planes[:, S + c : S + c + P])
+                k5_op = (k5_early[:, c : c + P], early_planes[:, S + W + c : S + W + c + P])
+            else:
+                k4_op = (late_codes[:, c : c + P], late_planes[:, c : c + P])
+                k5_op = (late_codes[:, W + c : W + c + P], late_planes[:, W + c : W + c + P])
+            bank = psum.tile([P, S], F32, name="h2_bank%d" % m)
+            nc.tensor.matmul_mx(
+                out=bank[:], lhsT=k5_op[0].bitcast(FP8X4), lhsT_scale=k5_op[1],
+                rhs=duo_codes[:].bitcast(FP8X4), rhs_scale=early_planes[:, 0:S], start=True, stop=False,
+            )
+            nc.tensor.matmul_mx(
+                out=bank[:], lhsT=k4_op[0].bitcast(FP8X4), lhsT_scale=k4_op[1],
+                rhs=z_codes[:].bitcast(FP8X4), rhs_scale=z_plane[:], start=False, stop=True,
+            )
+            h2 = keep.tile([P, S], F32, name="h2_%d" % m, tag="window", align_bytes=64)
+            nc.scalar.activation(h2[:], bank[:], COPY, scale=0.0625)
+            pa2.append(new("pa2_%d" % m, W, F32))
+            nb2.append(new("nb2_%d" % m, W, F32))
+            nc.scalar.activation(pa2[m][:], h2[:].indirect(whole("n6")), COPY)
+            nc.scalar.activation(nb2[m][:], h2[:].indirect(whole("n7")), COPY, scale=-1.0)
+
+        res = [new("res%d" % m, S, F32) for m in range(4)]
+        ra2 = [new("ra2_%d" % m, W, F32) for m in range(4)]
+
+        def larger(m):
+            nc.vector.scalar_tensor_tensor(ra2[m][:], nb2[m][:], -1.0, pa2[m][:], ALU.mult, ALU.max)
+
+        def put_difference(m):
+            nc.vector.tensor_tensor(res[m][:].indirect(whole("n9")), pa2[m][:], nb2[m][:], ALU.add)
+
+        def put_larger(m):
+            nc.vector.tensor_copy(res[m][:].indirect(whole("n8")), ra2[m][:])
+            nc.sync.dma_start(out=out[m * P : (m + 1) * P, :], in_=res[m][:])
+
+        larger(0)
+        put_difference(0)
+        for m in range(1, 4):
+            larger(m)
+            put_difference(m)
+            put_larger(m - 1)
+        put_larger(3)

@@ -1,6 +1,7 @@
 from contextlib import ExitStack
 
 import concourse.mybir as mybir
+from concourse.masks import make_identity
 
 F32 = mybir.dt.float32
 BF16 = mybir.dt.bfloat16
@@ -74,6 +75,11 @@ def tile_picked_mtthzmtcpsdcpmx_none_p_kernel(
         for plane in (x_planes, k_packed, early_planes, late_planes):
             nc.vector.memset(plane[:].bitcast(I32), 0)
 
+        minus_one = new("minus_one", S, F32)
+        nc.vector.memset(minus_one[:], -1.0)
+        identity = new("identity", P, F32)
+        make_identity(nc, identity[:])
+
         x_names = ("offs", "two", "hz")
         k_names = ("k1", "k2", "k3")
         for a, name in enumerate(k_names):
@@ -109,7 +115,7 @@ def tile_picked_mtthzmtcpsdcpmx_none_p_kernel(
         gather(x_codes[1][:], x_table, whole("two"))
         gather(x_codes[2][:], x_table, whole("hz"))
 
-        h_banks = [psum.tile([P, S], F32, name="h_bank%d" % t) for t in range(4)]
+        h_banks = [psum.tile([P, S], F32, name="h_bank%d" % t, tag="bank%d" % t) for t in range(4)]
         for t in range(4):
             cols = slice(t * P, (t + 1) * P)
             for a in range(3):
@@ -123,39 +129,80 @@ def tile_picked_mtthzmtcpsdcpmx_none_p_kernel(
                     stop=(a == 2),
                 )
 
-        pa, pb = [], []
+        def block_tiles(name):
+            first, rest = new(name + "_first", W, F32), new(name + "_rest", 3 * W, F32)
+            return first, rest, [first[:]] + [rest[:, t * W : (t + 1) * W] for t in range(3)]
+
+        def pieces(t):
+            return [(0, W // 2), (W // 2, W)] if t == 0 else [(0, W)]
+
+        def entries(name, lo, hi):
+            return lists[name][:, lo // 16 : hi // 16]
+
+        def fetch_pairs(bank, t, name, left, left_list, right, right_list, right_sign):
+            window = keep.tile([P, S], F32, name=name, tag="window", align_bytes=64)
+            nc.scalar.activation(window[:], bank[:], COPY, scale=0.0625)
+            for lo, hi in pieces(t):
+                nc.scalar.activation(left[:, lo:hi], window[:].indirect(entries(left_list, lo, hi)), COPY)
+                nc.scalar.activation(right[:, lo:hi], window[:].indirect(entries(right_list, lo, hi)), COPY, scale=right_sign)
+
+        pa_first, pa_rest, pa = block_tiles("pa")
+        pb_first, pb_rest, pb = block_tiles("pb")
+        ra_first, ra_rest, ra = block_tiles("ra")
         for t in range(4):
-            h = keep.tile([P, S], F32, name="h%d" % t, tag="window", align_bytes=64)
-            nc.scalar.activation(h[:], h_banks[t][:], COPY, scale=0.0625)
-            pa.append(new("pa%d" % t, W, F32))
-            pb.append(new("pb%d" % t, W, F32))
-            nc.scalar.activation(pa[t][:], h[:].indirect(whole("n1")), COPY)
-            nc.scalar.activation(pb[t][:], h[:].indirect(whole("n2")), COPY)
+            fetch_pairs(h_banks[t], t, "h%d" % t, pa[t], "n1", pb[t], "n2", 1.0)
 
         ub = [new("ub%d" % t, S, F32) for t in range(3)] + [placed("ub3", S, F32, 2048)]
         ds = [new("ds%d" % t, 2 * S, F32) for t in range(3)] + [placed("ds3", 2 * S, F32, 4096)]
-        diff = [new("diff%d" % t, S, F32) for t in range(3)] + [placed("diff3", S, F32, 12288)]
+        diff_last = placed("diff_last", S, F32, 0)
         z = placed("z", 4 * S, BF16, 8192)
         z_by_slot = z[:].rearrange("p (j t) -> p j t", t=4)
 
-        def send(t):
+        def put_sum(t, lo=0, hi=W):
+            nc.vector.tensor_tensor(ub[t][:].indirect(entries("n4", lo, hi)), pa[t][:, lo:hi], pb[t][:, lo:hi], ALU.add)
+
+        def put_smaller(t):
+            nc.vector.tensor_copy(ub[t][:].indirect(whole("n3")), ra[t])
+
+        def write_z(t, difference):
+            nc.scalar.activation(z_by_slot[:, :, t], difference, COPY, scale=gain[:, t : t + 1])
+
+        def finish_on_tensor(t):
+            nc.vector.tensor_tensor(ds[t][:].indirect(whole("n5")), ub[t][:], minus_one[:], ALU.mult)
+            turned = psum.tile([P, S], F32, name="turned%d" % t, tag="bank4")
+            for b in range(0, S, P):
+                for source, first in ((ub[t], True), (ds[t], False)):
+                    nc.tensor.matmul(
+                        turned[:, b : b + P], source[:, b : b + P], identity[:], start=first, stop=not first, is_transpose=True
+                    )
+            staged = reuse.tile([P, S], F32, name="staged%d" % t, tag="staged", align_bytes=64, offset=0)
+            nc.scalar.copy(staged[:], turned[:])
+            back = psum.tile([P, S], F32, name="back%d" % t, tag="bank5")
+            for b in range(0, S, P):
+                nc.tensor.transpose(back[:, b : b + P], staged[:, b : b + P], identity[:])
+            write_z(t, back[:])
+
+        def finish_on_vector(t):
             nc.vector.tensor_copy(ds[t][:].indirect(whole("n5")), ub[t][:])
+            nc.vector.tensor_tensor(diff_last[:], ub[t][:], ds[t][:, 0:S], ALU.subtract)
+            write_z(t, diff_last[:])
 
-        def finish(t):
-            nc.vector.tensor_tensor(diff[t][:], ub[t][:], ds[t][:, 0:S], ALU.subtract)
-            nc.scalar.activation(z_by_slot[:, :, t], diff[t][:], COPY, scale=gain[:, t : t + 1])
-
-        for t in range(4):
-            ra = new("ra%d" % t, W, F32)
-            nc.vector.tensor_tensor(ra[:], pa[t][:], pb[t][:], ALU.min)
-            nc.vector.tensor_tensor(ub[t][:].indirect(whole("n4")), pa[t][:], pb[t][:], ALU.add)
-            if t > 0:
-                send(t - 1)
-            nc.vector.tensor_copy(ub[t][:].indirect(whole("n3")), ra[:])
-            if t > 0:
-                finish(t - 1)
-        send(3)
-        finish(3)
+        put_sum(0, 0, W // 2)
+        nc.vector.tensor_tensor(ra[0], pa[0], pb[0], ALU.min)
+        put_sum(0, W // 2, W)
+        put_smaller(0)
+        nc.vector.tensor_tensor(ra[1], pa[1], pb[1], ALU.min)
+        put_sum(1)
+        finish_on_tensor(0)
+        put_smaller(1)
+        put_sum(2)
+        nc.vector.tensor_tensor(ra_rest[:, W:], pa_rest[:, W:], pb_rest[:, W:], ALU.min)
+        put_sum(3)
+        put_smaller(2)
+        finish_on_tensor(1)
+        finish_on_tensor(2)
+        put_smaller(3)
+        finish_on_vector(3)
         z_codes = new("z_codes", S, U32)
         z_plane = new("z_plane", S, U8)
         nc.vector.quantize_mx(out=z_codes[:].bitcast(FP8X4), scales=z_plane[:], in_=z[:])
@@ -171,7 +218,7 @@ def tile_picked_mtthzmtcpsdcpmx_none_p_kernel(
         gather(duo_codes[:], x_table, whole("duo"))
         k5_early = placed("k5_early", W, U32, 4096)
         gather(k5_early[:], d_table, half("k5", 0))
-        late_got = placed("late_got", 2 * W, U8, 12288)
+        late_got = placed("late_got", 2 * W, U8, 0)
         gather(late_got[:, 0:W], d_bytes, half("k4", 1))
         gather(late_got[:, W : 2 * W], d_bytes, half("k5", 1))
         place_rows(nc.sync, late_planes, 0, late_got)
@@ -179,7 +226,9 @@ def tile_picked_mtthzmtcpsdcpmx_none_p_kernel(
         gather(late_codes[:, 0:W], d_table, half("k4", 1))
         gather(late_codes[:, W : 2 * W], d_table, half("k5", 1))
 
-        pa2, nb2 = [], []
+        pa2_first, pa2_rest, pa2 = block_tiles("pa2")
+        nb2_first, nb2_rest, nb2 = block_tiles("nb2")
+        ra2_first, ra2_rest, ra2 = block_tiles("ra2")
         for m in range(4):
             c = (m % 2) * P
             if m < 2:
@@ -188,7 +237,7 @@ def tile_picked_mtthzmtcpsdcpmx_none_p_kernel(
             else:
                 k4_op = (late_codes[:, c : c + P], late_planes[:, c : c + P])
                 k5_op = (late_codes[:, W + c : W + c + P], late_planes[:, W + c : W + c + P])
-            bank = psum.tile([P, S], F32, name="h2_bank%d" % m)
+            bank = psum.tile([P, S], F32, name="h2_bank%d" % m, tag="bank%d" % ((6 + m) % 8))
             nc.tensor.matmul_mx(
                 out=bank[:], lhsT=k5_op[0].bitcast(FP8X4), lhsT_scale=k5_op[1],
                 rhs=duo_codes[:].bitcast(FP8X4), rhs_scale=early_planes[:, 0:S], start=True, stop=False,
@@ -197,30 +246,29 @@ def tile_picked_mtthzmtcpsdcpmx_none_p_kernel(
                 out=bank[:], lhsT=k4_op[0].bitcast(FP8X4), lhsT_scale=k4_op[1],
                 rhs=z_codes[:].bitcast(FP8X4), rhs_scale=z_plane[:], start=False, stop=True,
             )
-            h2 = keep.tile([P, S], F32, name="h2_%d" % m, tag="window", align_bytes=64)
-            nc.scalar.activation(h2[:], bank[:], COPY, scale=0.0625)
-            pa2.append(new("pa2_%d" % m, W, F32))
-            nb2.append(new("nb2_%d" % m, W, F32))
-            nc.scalar.activation(pa2[m][:], h2[:].indirect(whole("n6")), COPY)
-            nc.scalar.activation(nb2[m][:], h2[:].indirect(whole("n7")), COPY, scale=-1.0)
+            fetch_pairs(bank, m, "h2_%d" % m, pa2[m], "n6", nb2[m], "n7", -1.0)
 
         res = [new("res%d" % m, S, F32) for m in range(4)]
-        ra2 = [new("ra2_%d" % m, W, F32) for m in range(4)]
 
-        def larger(m):
-            nc.vector.scalar_tensor_tensor(ra2[m][:], nb2[m][:], -1.0, pa2[m][:], ALU.mult, ALU.max)
-
-        def put_difference(m):
-            nc.vector.tensor_tensor(res[m][:].indirect(whole("n9")), pa2[m][:], nb2[m][:], ALU.add)
+        def put_difference(m, lo=0, hi=W):
+            nc.vector.tensor_tensor(res[m][:].indirect(entries("n9", lo, hi)), pa2[m][:, lo:hi], nb2[m][:, lo:hi], ALU.add)
 
         def put_larger(m):
-            nc.vector.tensor_copy(res[m][:].indirect(whole("n8")), ra2[m][:])
+            nc.vector.tensor_copy(res[m][:].indirect(whole("n8")), ra2[m])
             nc.sync.dma_start(out=out[m * P : (m + 1) * P, :], in_=res[m][:])
 
-        larger(0)
-        put_difference(0)
-        for m in range(1, 4):
-            larger(m)
-            put_difference(m)
-            put_larger(m - 1)
+        def larger(dst, negated, plain):
+            nc.vector.scalar_tensor_tensor(dst, negated, -1.0, plain, ALU.mult, ALU.max)
+
+        put_difference(0, 0, W // 2)
+        larger(ra2[0], nb2[0], pa2[0])
+        put_difference(0, W // 2, W)
+        put_larger(0)
+        larger(ra2[1], nb2[1], pa2[1])
+        put_difference(1)
+        put_larger(1)
+        put_difference(2)
+        larger(ra2_rest[:, W:], nb2_rest[:, W:], pa2_rest[:, W:])
+        put_difference(3)
+        put_larger(2)
         put_larger(3)

@@ -18,7 +18,16 @@ S = 512
 W = 256
 T = 1024
 G = 2048
+BLOCKS = 4
+SIXTEENTH = 0.0625
 FLOPS = 5 * 2 * 512 * 512 * 512
+
+AT_TURNED = 0
+AT_UB_LAST = AT_TURNED + 4 * S
+AT_DS_LAST = AT_UB_LAST + 4 * S
+AT_Z = AT_DS_LAST + 8 * S
+AT_RAW = AT_Z + 8 * S
+AT_K = AT_RAW + 12 * S
 
 
 def tile_picked_mtthzmtcpsdcpmx_none_p_kernel(
@@ -27,84 +36,92 @@ def tile_picked_mtthzmtcpsdcpmx_none_p_kernel(
     nc = tc.nc
     with ExitStack() as ctx:
         keep = ctx.enter_context(tc.tile_pool(name="keep", bufs=1))
-        reuse = ctx.enter_context(tc.tile_pool(name="reuse", bufs=1))
+        shared = ctx.enter_context(tc.tile_pool(name="shared", bufs=1))
         psum = ctx.enter_context(tc.psum_pool(name="psum", bufs=1))
 
         def new(name, cols, dtype):
             return keep.tile([P, cols], dtype, name=name, align_bytes=64)
 
         def placed(name, cols, dtype, offset):
-            return reuse.tile([P, cols], dtype, name=name, align_bytes=64, offset=offset)
+            return shared.tile([P, cols], dtype, name=name, align_bytes=64, offset=offset)
+
+        def bank(name, number):
+            return psum.tile([P, S], F32, name=name, tag="bank%d" % number)
 
         x_bytes = new("x_bytes", T, U8)
         d_bytes = new("d_bytes", G, U8)
         x_table = new("x_table", T, U32)
         d_table = new("d_table", G, U32)
-        for tile_, src, cols in ((d_bytes, d_scales, G), (x_bytes, x_scales, T)):
-            rows = src[0].bitcast(I32)
-            nc.scalar.dma_start(out=tile_[:].bitcast(I32), in_=rows.unsqueeze(1).to_broadcast([16, 8, cols // 4]))
-        for tile_, src in ((d_table, d_words), (x_table, x_words)):
-            nc.scalar.dma_start(out=tile_[:].bitcast(I32), in_=src[0].rearrange("p n t -> p (n t)").bitcast(I32))
+        for table, scales, cols in ((x_bytes, x_scales, T), (d_bytes, d_scales, G)):
+            rows = scales[0].bitcast(I32)
+            nc.scalar.dma_start(out=table[:].bitcast(I32), in_=rows.unsqueeze(1).to_broadcast([16, 8, cols // 4]))
+        for table, words in ((d_table, d_words), (x_table, x_words)):
+            nc.scalar.dma_start(out=table[:].bitcast(I32), in_=words[0].rearrange("p n t -> p (n t)").bitcast(I32))
 
         lists = {}
 
         def load_lists(*named):
-            for name, src in named:
-                lists[name] = keep.tile([P, src.shape[1]], U16, name="list_" + name)
-                nc.sync.dma_start(lists[name][:], src)
-
-        load_lists(("k1", k1), ("k2", k2), ("k3", k3), ("offs", offs), ("two", two), ("hz", hz))
+            for name, source in named:
+                lists[name] = keep.tile([P, source.shape[1]], U16, name="list_" + name)
+                nc.sync.dma_start(lists[name][:], source)
 
         def whole(name):
             return lists[name][:]
 
-        def half(name, h):
-            return lists[name][:, 16 * h : 16 * (h + 1)]
+        def entries(name, lo, hi):
+            return lists[name][:, lo // 16 : hi // 16]
 
         def gather(dst, table, offsets):
             nc.vector.tensor_copy(dst, table[:].indirect(offsets))
 
         def place_rows(queue, plane, first, gathered):
             for q in range(0, P, 32):
-                queue.dma_start(out=plane[q + first : q + first + 4, :].bitcast(I32), in_=gathered[q : q + 32 : 8, :].bitcast(I32))
+                queue.dma_start(
+                    out=plane[q + first : q + first + 4, :].bitcast(I32), in_=gathered[q : q + 32 : 8, :].bitcast(I32)
+                )
+
+        load_lists(("offs", offs), ("k1", k1), ("k2", k2), ("k3", k3), ("two", two), ("hz", hz))
 
         x_planes = new("x_planes", 3 * S, U8)
-        k_packed = placed("k_packed", S, U8, 14336 + 6144)
+        k_packed = placed("k_packed", S, U8, AT_K)
         early_planes = new("early_planes", S + 2 * W, U8)
         late_planes = new("late_planes", 2 * W, U8)
         for plane in (x_planes, k_packed, early_planes, late_planes):
             nc.vector.memset(plane[:].bitcast(I32), 0)
-
         minus_one = new("minus_one", S, F32)
         nc.vector.memset(minus_one[:], -1.0)
         identity = new("identity", P, F32)
         make_identity(nc, identity[:])
 
-        x_names = ("offs", "two", "hz")
         k_names = ("k1", "k2", "k3")
+        x_got = new("x_got", 3 * S, U8)
+        gather(x_got[:, 0:S], x_bytes, whole("offs"))
         for a, name in enumerate(k_names):
             k_got = new("k_got%d" % a, S, U8)
             gather(k_got[:], d_bytes, whole(name))
             place_rows(nc.sync, k_packed, 4 * a, k_got)
-        x_got = new("x_got", 3 * S, U8)
-        for a, name in enumerate(x_names):
-            gather(x_got[:, a * S : (a + 1) * S], x_bytes, whole(name))
+        gather(x_got[:, S : 2 * S], x_bytes, whole("two"))
+        gather(x_got[:, 2 * S : 3 * S], x_bytes, whole("hz"))
         place_rows(nc.scalar, x_planes, 0, x_got)
 
         load_lists(("duo", duo), ("k4", k4), ("k5", k5), ("n1", n1), ("n2", n2), ("n4", n4), ("n3", n3), ("n5", n5))
-        gain = new("gain", 4, F32)
-        nc.sync.dma_start(out=gain[:], in_=gs.rearrange("(p t) o -> p (t o)", t=4))
+        gain = new("gain", BLOCKS, F32)
+        nc.sync.dma_start(out=gain[:], in_=gs.rearrange("(p t) o -> p (t o)", t=BLOCKS))
         load_lists(("n6", n6), ("n7", n7), ("n9", n9), ("n8", n8))
 
-        raw = placed("raw", 3 * S, U32, 14336)
-        k_codes = new("k_codes", 3 * S, U32)
-        x_codes = [new("x_codes0", S, U32), placed("x_codes1", S, U32, 14336 + 4352), placed("x_codes2", S, U32, 14336 + 6400)]
+        raw = placed("raw", 3 * S, U32, AT_RAW)
+        k_codes = placed("k_codes", 3 * S, U32, AT_K)
         k_planes = new("k_planes", S, U8)
+        x_codes = [
+            new("offs_codes", S, U32),
+            placed("two_codes", S, U32, AT_RAW + 4 * S),
+            placed("hz_codes", S, U32, AT_RAW + 8 * S),
+        ]
 
         def deal(dst, src, run):
             nc.vector.tensor_copy(
-                dst[:].rearrange("p (t c i) -> p c t i", t=4, i=run),
-                src[:].rearrange("p (c i t) -> p c t i", t=4, i=run),
+                dst[:].rearrange("p (t c i) -> p c t i", t=BLOCKS, i=run),
+                src[:].rearrange("p (c i t) -> p c t i", t=BLOCKS, i=run),
             )
 
         for a, name in enumerate(k_names):
@@ -115,48 +132,41 @@ def tile_picked_mtthzmtcpsdcpmx_none_p_kernel(
         gather(x_codes[1][:], x_table, whole("two"))
         gather(x_codes[2][:], x_table, whole("hz"))
 
-        h_banks = [psum.tile([P, S], F32, name="h_bank%d" % t, tag="bank%d" % t) for t in range(4)]
-        for t in range(4):
-            cols = slice(t * P, (t + 1) * P)
+        h_banks = [bank("h_bank%d" % t, t) for t in range(BLOCKS)]
+        for t in range(BLOCKS):
             for a in range(3):
                 nc.tensor.matmul_mx(
                     out=h_banks[t][:],
                     lhsT=k_codes[:, (3 * t + a) * P : (3 * t + a + 1) * P].bitcast(FP8X4),
-                    lhsT_scale=k_planes[4 * a : P, cols],
+                    lhsT_scale=k_planes[4 * a : P, t * P : (t + 1) * P],
                     rhs=x_codes[a][:].bitcast(FP8X4),
                     rhs_scale=x_planes[:, a * S : (a + 1) * S],
                     start=(a == 0),
                     stop=(a == 2),
                 )
 
-        def block_tiles(name):
-            first, rest = new(name + "_first", W, F32), new(name + "_rest", 3 * W, F32)
-            return first, rest, [first[:]] + [rest[:, t * W : (t + 1) * W] for t in range(3)]
+        def pair_tiles(name):
+            tiles = [new(name + "0", W, F32), new(name + "1", W, F32), new(name + "23", 2 * W, F32)]
+            return [tiles[0][:], tiles[1][:], tiles[2][:, 0:W], tiles[2][:, W : 2 * W]], tiles[2][:]
 
-        def pieces(t):
-            return [(0, W // 2), (W // 2, W)] if t == 0 else [(0, W)]
-
-        def entries(name, lo, hi):
-            return lists[name][:, lo // 16 : hi // 16]
-
-        def fetch_pairs(bank, t, name, left, left_list, right, right_list, right_sign):
+        def fetch_pairs(name, source, block, left, left_list, right, right_list, right_sign):
             window = keep.tile([P, S], F32, name=name, tag="window", align_bytes=64)
-            nc.scalar.activation(window[:], bank[:], COPY, scale=0.0625)
-            for lo, hi in pieces(t):
+            nc.scalar.activation(window[:], source[:], COPY, scale=SIXTEENTH)
+            for lo, hi in [(0, W // 2), (W // 2, W)] if block == 0 else [(0, W)]:
                 nc.scalar.activation(left[:, lo:hi], window[:].indirect(entries(left_list, lo, hi)), COPY)
                 nc.scalar.activation(right[:, lo:hi], window[:].indirect(entries(right_list, lo, hi)), COPY, scale=right_sign)
 
-        pa_first, pa_rest, pa = block_tiles("pa")
-        pb_first, pb_rest, pb = block_tiles("pb")
-        ra_first, ra_rest, ra = block_tiles("ra")
-        for t in range(4):
-            fetch_pairs(h_banks[t], t, "h%d" % t, pa[t], "n1", pb[t], "n2", 1.0)
+        pa, pa_23 = pair_tiles("pa")
+        pb, pb_23 = pair_tiles("pb")
+        ra, ra_23 = pair_tiles("ra")
+        for t in range(BLOCKS):
+            fetch_pairs("h%d" % t, h_banks[t], t, pa[t], "n1", pb[t], "n2", 1.0)
 
-        ub = [new("ub%d" % t, S, F32) for t in range(3)] + [placed("ub3", S, F32, 2048)]
-        ds = [new("ds%d" % t, 2 * S, F32) for t in range(3)] + [placed("ds3", 2 * S, F32, 4096)]
-        diff_last = placed("diff_last", S, F32, 0)
-        z = placed("z", 4 * S, BF16, 8192)
-        z_by_slot = z[:].rearrange("p (j t) -> p j t", t=4)
+        last = BLOCKS - 1
+        ub = [new("ub%d" % t, S, F32) for t in range(last)] + [placed("ub_last", S, F32, AT_UB_LAST)]
+        ds = [new("ds%d" % t, 2 * S, F32) for t in range(last)] + [placed("ds_last", 2 * S, F32, AT_DS_LAST)]
+        z = placed("z", BLOCKS * S, BF16, AT_Z)
+        z_by_block = z[:].rearrange("p (j t) -> p j t", t=BLOCKS)
 
         def put_sum(t, lo=0, hi=W):
             nc.vector.tensor_tensor(ub[t][:].indirect(entries("n4", lo, hi)), pa[t][:, lo:hi], pb[t][:, lo:hi], ALU.add)
@@ -165,27 +175,28 @@ def tile_picked_mtthzmtcpsdcpmx_none_p_kernel(
             nc.vector.tensor_copy(ub[t][:].indirect(whole("n3")), ra[t])
 
         def write_z(t, difference):
-            nc.scalar.activation(z_by_slot[:, :, t], difference, COPY, scale=gain[:, t : t + 1])
+            nc.scalar.activation(z_by_block[:, :, t], difference, COPY, scale=gain[:, t : t + 1])
 
         def finish_on_tensor(t):
             nc.vector.tensor_tensor(ds[t][:].indirect(whole("n5")), ub[t][:], minus_one[:], ALU.mult)
-            turned = psum.tile([P, S], F32, name="turned%d" % t, tag="bank4")
-            for b in range(0, S, P):
-                for source, first in ((ub[t], True), (ds[t], False)):
+            summed = bank("summed%d" % t, 4)
+            for c in range(0, S, P):
+                for source, opens in ((ub[t], True), (ds[t], False)):
                     nc.tensor.matmul(
-                        turned[:, b : b + P], source[:, b : b + P], identity[:], start=first, stop=not first, is_transpose=True
+                        summed[:, c : c + P], source[:, c : c + P], identity[:], start=opens, stop=not opens, is_transpose=True
                     )
-            staged = reuse.tile([P, S], F32, name="staged%d" % t, tag="staged", align_bytes=64, offset=0)
-            nc.scalar.copy(staged[:], turned[:])
-            back = psum.tile([P, S], F32, name="back%d" % t, tag="bank5")
-            for b in range(0, S, P):
-                nc.tensor.transpose(back[:, b : b + P], staged[:, b : b + P], identity[:])
+            turned = shared.tile([P, S], F32, name="turned%d" % t, tag="turned", align_bytes=64, offset=AT_TURNED)
+            nc.scalar.copy(turned[:], summed[:])
+            back = bank("back%d" % t, 5)
+            for c in range(0, S, P):
+                nc.tensor.transpose(back[:, c : c + P], turned[:, c : c + P], identity[:])
             write_z(t, back[:])
 
         def finish_on_vector(t):
             nc.vector.tensor_copy(ds[t][:].indirect(whole("n5")), ub[t][:])
-            nc.vector.tensor_tensor(diff_last[:], ub[t][:], ds[t][:, 0:S], ALU.subtract)
-            write_z(t, diff_last[:])
+            difference = placed("difference", S, F32, AT_TURNED)
+            nc.vector.tensor_tensor(difference[:], ub[t][:], ds[t][:, 0:S], ALU.subtract)
+            write_z(t, difference[:])
 
         put_sum(0, 0, W // 2)
         nc.vector.tensor_tensor(ra[0], pa[0], pb[0], ALU.min)
@@ -196,7 +207,7 @@ def tile_picked_mtthzmtcpsdcpmx_none_p_kernel(
         finish_on_tensor(0)
         put_smaller(1)
         put_sum(2)
-        nc.vector.tensor_tensor(ra_rest[:, W:], pa_rest[:, W:], pb_rest[:, W:], ALU.min)
+        nc.vector.tensor_tensor(ra_23, pa_23, pb_23, ALU.min)
         put_sum(3)
         put_smaller(2)
         finish_on_tensor(1)
@@ -207,68 +218,71 @@ def tile_picked_mtthzmtcpsdcpmx_none_p_kernel(
         z_plane = new("z_plane", S, U8)
         nc.vector.quantize_mx(out=z_codes[:].bitcast(FP8X4), scales=z_plane[:], in_=z[:])
 
-        early_got = placed("early_got", S + 2 * W, U8, 14336)
+        early_got = placed("early_got", S + 2 * W, U8, AT_RAW)
         gather(early_got[:, 0:S], x_bytes, whole("duo"))
-        gather(early_got[:, S : S + W], d_bytes, half("k4", 0))
-        gather(early_got[:, S + W : S + 2 * W], d_bytes, half("k5", 0))
+        gather(early_got[:, S : S + W], d_bytes, entries("k4", 0, W))
+        gather(early_got[:, S + W : S + 2 * W], d_bytes, entries("k5", 0, W))
         place_rows(nc.sync, early_planes, 0, early_got)
-        k4_early = placed("k4_early", W, U32, 14336 + 1024)
-        gather(k4_early[:], d_table, half("k4", 0))
-        duo_codes = placed("duo_codes", S, U32, 2048)
+        k4_early = placed("k4_early", W, U32, AT_RAW + 2 * S)
+        gather(k4_early[:], d_table, entries("k4", 0, W))
+        duo_codes = placed("duo_codes", S, U32, AT_UB_LAST)
         gather(duo_codes[:], x_table, whole("duo"))
-        k5_early = placed("k5_early", W, U32, 4096)
-        gather(k5_early[:], d_table, half("k5", 0))
-        late_got = placed("late_got", 2 * W, U8, 0)
-        gather(late_got[:, 0:W], d_bytes, half("k4", 1))
-        gather(late_got[:, W : 2 * W], d_bytes, half("k5", 1))
+        k5_early = placed("k5_early", W, U32, AT_DS_LAST)
+        gather(k5_early[:], d_table, entries("k5", 0, W))
+        late_got = placed("late_got", 2 * W, U8, AT_TURNED)
+        gather(late_got[:, 0:W], d_bytes, entries("k4", W, S))
+        gather(late_got[:, W : 2 * W], d_bytes, entries("k5", W, S))
         place_rows(nc.sync, late_planes, 0, late_got)
-        late_codes = placed("late_codes", 2 * W, U32, 8192)
-        gather(late_codes[:, 0:W], d_table, half("k4", 1))
-        gather(late_codes[:, W : 2 * W], d_table, half("k5", 1))
+        late_codes = placed("late_codes", 2 * W, U32, AT_Z)
+        gather(late_codes[:, 0:W], d_table, entries("k4", W, S))
+        gather(late_codes[:, W : 2 * W], d_table, entries("k5", W, S))
 
-        pa2_first, pa2_rest, pa2 = block_tiles("pa2")
-        nb2_first, nb2_rest, nb2 = block_tiles("nb2")
-        ra2_first, ra2_rest, ra2 = block_tiles("ra2")
-        for m in range(4):
-            c = (m % 2) * P
-            if m < 2:
-                k4_op = (k4_early[:, c : c + P], early_planes[:, S + c : S + c + P])
-                k5_op = (k5_early[:, c : c + P], early_planes[:, S + W + c : S + W + c + P])
-            else:
-                k4_op = (late_codes[:, c : c + P], late_planes[:, c : c + P])
-                k5_op = (late_codes[:, W + c : W + c + P], late_planes[:, W + c : W + c + P])
-            bank = psum.tile([P, S], F32, name="h2_bank%d" % m, tag="bank%d" % ((6 + m) % 8))
-            nc.tensor.matmul_mx(
-                out=bank[:], lhsT=k5_op[0].bitcast(FP8X4), lhsT_scale=k5_op[1],
-                rhs=duo_codes[:].bitcast(FP8X4), rhs_scale=early_planes[:, 0:S], start=True, stop=False,
+        k4_halves = [(k4_early[:], early_planes[:, S : S + W]), (late_codes[:, 0:W], late_planes[:, 0:W])]
+        k5_halves = [(k5_early[:], early_planes[:, S + W : S + 2 * W]), (late_codes[:, W : 2 * W], late_planes[:, W : 2 * W])]
+        h2_bank_numbers = (6, 7, 0, 1)
+        pa2, pa2_23 = pair_tiles("pa2_")
+        nb2, nb2_23 = pair_tiles("nb2_")
+        ra2, ra2_23 = pair_tiles("ra2_")
+        for m in range(BLOCKS):
+            cols = slice((m % 2) * P, (m % 2 + 1) * P)
+            h2_bank = bank("h2_bank%d" % m, h2_bank_numbers[m])
+            passes = (
+                (k5_halves[m // 2], duo_codes[:], early_planes[:, 0:S]),
+                (k4_halves[m // 2], z_codes[:], z_plane[:]),
             )
-            nc.tensor.matmul_mx(
-                out=bank[:], lhsT=k4_op[0].bitcast(FP8X4), lhsT_scale=k4_op[1],
-                rhs=z_codes[:].bitcast(FP8X4), rhs_scale=z_plane[:], start=False, stop=True,
-            )
-            fetch_pairs(bank, m, "h2_%d" % m, pa2[m], "n6", nb2[m], "n7", -1.0)
+            for a, ((codes, plane), moving, moving_plane) in enumerate(passes):
+                nc.tensor.matmul_mx(
+                    out=h2_bank[:],
+                    lhsT=codes[:, cols].bitcast(FP8X4),
+                    lhsT_scale=plane[:, cols],
+                    rhs=moving.bitcast(FP8X4),
+                    rhs_scale=moving_plane,
+                    start=(a == 0),
+                    stop=(a == 1),
+                )
+            fetch_pairs("h2_%d" % m, h2_bank, m, pa2[m], "n6", nb2[m], "n7", -1.0)
 
-        res = [new("res%d" % m, S, F32) for m in range(4)]
-
-        def put_difference(m, lo=0, hi=W):
-            nc.vector.tensor_tensor(res[m][:].indirect(entries("n9", lo, hi)), pa2[m][:, lo:hi], nb2[m][:, lo:hi], ALU.add)
-
-        def put_larger(m):
-            nc.vector.tensor_copy(res[m][:].indirect(whole("n8")), ra2[m])
-            nc.sync.dma_start(out=out[m * P : (m + 1) * P, :], in_=res[m][:])
+        result = [new("result%d" % m, S, F32) for m in range(BLOCKS)]
 
         def larger(dst, negated, plain):
             nc.vector.scalar_tensor_tensor(dst, negated, -1.0, plain, ALU.mult, ALU.max)
 
+        def put_difference(m, lo=0, hi=W):
+            nc.vector.tensor_tensor(result[m][:].indirect(entries("n9", lo, hi)), pa2[m][:, lo:hi], nb2[m][:, lo:hi], ALU.add)
+
+        def put_larger_and_store(m):
+            nc.vector.tensor_copy(result[m][:].indirect(whole("n8")), ra2[m])
+            nc.sync.dma_start(out=out[m * P : (m + 1) * P, :], in_=result[m][:])
+
         put_difference(0, 0, W // 2)
         larger(ra2[0], nb2[0], pa2[0])
         put_difference(0, W // 2, W)
-        put_larger(0)
+        put_larger_and_store(0)
         larger(ra2[1], nb2[1], pa2[1])
         put_difference(1)
-        put_larger(1)
+        put_larger_and_store(1)
         put_difference(2)
-        larger(ra2_rest[:, W:], nb2_rest[:, W:], pa2_rest[:, W:])
+        larger(ra2_23, nb2_23, pa2_23)
         put_difference(3)
-        put_larger(2)
-        put_larger(3)
+        put_larger_and_store(2)
+        put_larger_and_store(3)

@@ -223,12 +223,12 @@ def tile_picked_mtthzmtcpsdcpmx_none_p_kernel(
         gather(early_got[:, S : S + W], d_bytes, entries("k4", 0, W))
         gather(early_got[:, S + W : S + 2 * W], d_bytes, entries("k5", 0, W))
         place_rows(nc.sync, early_planes, 0, early_got)
-        k4_early = placed("k4_early", W, U32, AT_RAW + 2 * S)
-        gather(k4_early[:], d_table, entries("k4", 0, W))
         duo_codes = placed("duo_codes", S, U32, AT_UB_LAST)
         gather(duo_codes[:], x_table, whole("duo"))
         k5_early = placed("k5_early", W, U32, AT_DS_LAST)
         gather(k5_early[:], d_table, entries("k5", 0, W))
+        k4_early = placed("k4_early", W, U32, AT_DS_LAST + 2 * S)
+        gather(k4_early[:], d_table, entries("k4", 0, W))
         late_got = placed("late_got", 2 * W, U8, AT_TURNED)
         gather(late_got[:, 0:W], d_bytes, entries("k4", W, S))
         gather(late_got[:, W : 2 * W], d_bytes, entries("k5", W, S))

from contextlib import ExitStack

import concourse.mybir as mybir
from concourse.masks import make_identity

F32 = mybir.dt.float32
BF16 = mybir.dt.bfloat16
I32 = mybir.dt.int32
U32 = mybir.dt.uint32
U16 = mybir.dt.uint16
U8 = mybir.dt.uint8
FP8X4 = mybir.dt.float8_e4m3fn_x4
ALU = mybir.AluOpType
COPY = mybir.ActivationFunctionType.Copy

P = 128
S = 512
W = 256
T = 1024
G = 2048
BLOCKS = 4
SIXTEENTH = 0.0625
FLOPS = 5 * 2 * 512 * 512 * 512

AT_TURNED = 0
AT_UB_LAST = AT_TURNED + 4 * S
AT_DS_LAST = AT_UB_LAST + 4 * S
AT_Z = AT_DS_LAST + 8 * S
AT_RAW = AT_Z + 8 * S
AT_K = AT_RAW + 12 * S


def tile_picked_mtthzmtcpsdcpmx_none_p_kernel(
    tc, x_words, x_scales, d_words, d_scales, gs, offs, k1, two, k2, hz, k3, n1, n2, n3, n4, n5, k4, k5, duo, n6, n7, n8, n9, out
):
    nc = tc.nc
    with ExitStack() as ctx:
        keep = ctx.enter_context(tc.tile_pool(name="keep", bufs=1))
        shared = ctx.enter_context(tc.tile_pool(name="shared", bufs=1))
        psum = ctx.enter_context(tc.psum_pool(name="psum", bufs=1))

        def new(name, cols, dtype):
            return keep.tile([P, cols], dtype, name=name, align_bytes=64)

        def placed(name, cols, dtype, offset):
            return shared.tile([P, cols], dtype, name=name, align_bytes=64, offset=offset)

        def bank(name, number):
            return psum.tile([P, S], F32, name=name, tag="bank%d" % number)

        x_bytes = new("x_bytes", T, U8)
        d_bytes = new("d_bytes", G, U8)
        x_table = new("x_table", T, U32)
        d_table = new("d_table", G, U32)
        for table, scales, cols in ((x_bytes, x_scales, T), (d_bytes, d_scales, G)):
            rows = scales[0].bitcast(I32)
            nc.scalar.dma_start(out=table[:].bitcast(I32), in_=rows.unsqueeze(1).to_broadcast([16, 8, cols // 4]))
        for table, words in ((d_table, d_words), (x_table, x_words)):
            nc.scalar.dma_start(out=table[:].bitcast(I32), in_=words[0].rearrange("p n t -> p (n t)").bitcast(I32))

        lists = {}

        def load_lists(*named):
            for name, source in named:
                lists[name] = keep.tile([P, source.shape[1]], U16, name="list_" + name)
                nc.sync.dma_start(lists[name][:], source)

        def whole(name):
            return lists[name][:]

        def entries(name, lo, hi):
            return lists[name][:, lo // 16 : hi // 16]

        def gather(dst, table, offsets):
            nc.vector.tensor_copy(dst, table[:].indirect(offsets))

        def place_rows(queue, plane, first, gathered):
            for q in range(0, P, 32):
                queue.dma_start(
                    out=plane[q + first : q + first + 4, :].bitcast(I32), in_=gathered[q : q + 32 : 8, :].bitcast(I32)
                )

        load_lists(("offs", offs), ("k1", k1), ("k2", k2), ("k3", k3), ("two", two), ("hz", hz))

        x_planes = new("x_planes", 3 * S, U8)
        k_packed = placed("k_packed", S, U8, AT_K)
        early_planes = new("early_planes", S + 2 * W, U8)
        late_planes = new("late_planes", 2 * W, U8)
        for plane in (x_planes, k_packed, early_planes, late_planes):
            nc.vector.memset(plane[:].bitcast(I32), 0)
        minus_one = new("minus_one", S, F32)
        nc.vector.memset(minus_one[:], -1.0)
        identity = new("identity", P, F32)
        make_identity(nc, identity[:])

        k_names = ("k1", "k2", "k3")
        x_got = new("x_got", 3 * S, U8)
        gather(x_got[:, 0:S], x_bytes, whole("offs"))
        for a, name in enumerate(k_names):
            k_got = new("k_got%d" % a, S, U8)
            gather(k_got[:], d_bytes, whole(name))
            place_rows(nc.sync, k_packed, 4 * a, k_got)
        gather(x_got[:, S : 2 * S], x_bytes, whole("two"))
        gather(x_got[:, 2 * S : 3 * S], x_bytes, whole("hz"))
        place_rows(nc.scalar, x_planes, 0, x_got)

        load_lists(("duo", duo), ("k4", k4), ("k5", k5), ("n1", n1), ("n2", n2), ("n4", n4), ("n3", n3), ("n5", n5))
        gain = new("gain", BLOCKS, F32)
        nc.sync.dma_start(out=gain[:], in_=gs.rearrange("(p t) o -> p (t o)", t=BLOCKS))
        load_lists(("n6", n6), ("n7", n7), ("n9", n9), ("n8", n8))

        raw = placed("raw", 3 * S, U32, AT_RAW)
        k_codes = placed("k_codes", 3 * S, U32, AT_K)
        k_planes = new("k_planes", S, U8)
        x_codes = [
            new("offs_codes", S, U32),
            placed("two_codes", S, U32, AT_RAW + 4 * S),
            placed("hz_codes", S, U32, AT_RAW + 8 * S),
        ]

        def deal(dst, src, run):
            nc.vector.tensor_copy(
                dst[:].rearrange("p (t c i) -> p c t i", t=BLOCKS, i=run),
                src[:].rearrange("p (c i t) -> p c t i", t=BLOCKS, i=run),
            )

        for a, name in enumerate(k_names):
            gather(raw[:, a * S : (a + 1) * S], d_table, whole(name))
        deal(k_planes, k_packed, 16)
        gather(x_codes[0][:], x_table, whole("offs"))
        deal(k_codes, raw, 4)
        gather(x_codes[1][:], x_table, whole("two"))
        gather(x_codes[2][:], x_table, whole("hz"))

        h_banks = [bank("h_bank%d" % t, t) for t in range(BLOCKS)]
        for t in range(BLOCKS):
            for a in range(3):
                nc.tensor.matmul_mx(
                    out=h_banks[t][:],
                    lhsT=k_codes[:, (3 * t + a) * P : (3 * t + a + 1) * P].bitcast(FP8X4),
                    lhsT_scale=k_planes[4 * a : P, t * P : (t + 1) * P],
                    rhs=x_codes[a][:].bitcast(FP8X4),
                    rhs_scale=x_planes[:, a * S : (a + 1) * S],
                    start=(a == 0),
                    stop=(a == 2),
                )

        def pair_tiles(name):
            tiles = [new(name + "0", W, F32), new(name + "1", W, F32), new(name + "23", 2 * W, F32)]
            return [tiles[0][:], tiles[1][:], tiles[2][:, 0:W], tiles[2][:, W : 2 * W]], tiles[2][:]

        def fetch_pairs(name, source, block, left, left_list, right, right_list, right_sign):
            window = keep.tile([P, S], F32, name=name, tag="window", align_bytes=64)
            nc.scalar.activation(window[:], source[:], COPY, scale=SIXTEENTH)
            for lo, hi in [(0, W // 2), (W // 2, W)] if block == 0 else [(0, W)]:
                nc.scalar.activation(left[:, lo:hi], window[:].indirect(entries(left_list, lo, hi)), COPY)
                nc.scalar.activation(right[:, lo:hi], window[:].indirect(entries(right_list, lo, hi)), COPY, scale=right_sign)

        pa, pa_23 = pair_tiles("pa")
        pb, pb_23 = pair_tiles("pb")
        ra, ra_23 = pair_tiles("ra")
        for t in range(BLOCKS):
            fetch_pairs("h%d" % t, h_banks[t], t, pa[t], "n1", pb[t], "n2", 1.0)

        last = BLOCKS - 1
        ub = [new("ub%d" % t, S, F32) for t in range(last)] + [placed("ub_last", S, F32, AT_UB_LAST)]
        ds = [new("ds%d" % t, 2 * S, F32) for t in range(last)] + [placed("ds_last", 2 * S, F32, AT_DS_LAST)]
        z = placed("z", BLOCKS * S, BF16, AT_Z)
        z_by_block = z[:].rearrange("p (j t) -> p j t", t=BLOCKS)

        def put_sum(t, lo=0, hi=W):
            nc.vector.tensor_tensor(ub[t][:].indirect(entries("n4", lo, hi)), pa[t][:, lo:hi], pb[t][:, lo:hi], ALU.add)

        def put_smaller(t):
            nc.vector.tensor_copy(ub[t][:].indirect(whole("n3")), ra[t])

        def write_z(t, difference):
            nc.scalar.activation(z_by_block[:, :, t], difference, COPY, scale=gain[:, t : t + 1])

        def finish_on_tensor(t):
            nc.vector.tensor_tensor(ds[t][:].indirect(whole("n5")), ub[t][:], minus_one[:], ALU.mult)
            summed = bank("summed%d" % t, 4)
            for c in range(0, S, P):
                for source, opens in ((ub[t], True), (ds[t], False)):
                    nc.tensor.matmul(
                        summed[:, c : c + P], source[:, c : c + P], identity[:], start=opens, stop=not opens, is_transpose=True
                    )
            turned = shared.tile([P, S], F32, name="turned%d" % t, tag="turned", align_bytes=64, offset=AT_TURNED)
            nc.scalar.copy(turned[:], summed[:])
            back = bank("back%d" % t, 5)
            for c in range(0, S, P):
                nc.tensor.transpose(back[:, c : c + P], turned[:, c : c + P], identity[:])
            write_z(t, back[:])

        def finish_on_vector(t):
            nc.vector.tensor_copy(ds[t][:].indirect(whole("n5")), ub[t][:])
            difference = placed("difference", S, F32, AT_TURNED)
            nc.vector.tensor_tensor(difference[:], ub[t][:], ds[t][:, 0:S], ALU.subtract)
            write_z(t, difference[:])

        put_sum(0, 0, W // 2)
        nc.vector.tensor_tensor(ra[0], pa[0], pb[0], ALU.min)
        put_sum(0, W // 2, W)
        put_smaller(0)
        nc.vector.tensor_tensor(ra[1], pa[1], pb[1], ALU.min)
        put_sum(1)
        finish_on_tensor(0)
        put_smaller(1)
        put_sum(2)
        nc.vector.tensor_tensor(ra_23, pa_23, pb_23, ALU.min)
        put_sum(3)
        put_smaller(2)
        finish_on_tensor(1)
        finish_on_tensor(2)
        put_smaller(3)
        finish_on_vector(3)
        z_codes = new("z_codes", S, U32)
        z_plane = new("z_plane", S, U8)
        nc.vector.quantize_mx(out=z_codes[:].bitcast(FP8X4), scales=z_plane[:], in_=z[:])

        early_got = placed("early_got", S + 2 * W, U8, AT_RAW)
        gather(early_got[:, 0:S], x_bytes, whole("duo"))
        gather(early_got[:, S : S + W], d_bytes, entries("k4", 0, W))
        gather(early_got[:, S + W : S + 2 * W], d_bytes, entries("k5", 0, W))
        place_rows(nc.sync, early_planes, 0, early_got)
        duo_codes = placed("duo_codes", S, U32, AT_UB_LAST)
        gather(duo_codes[:], x_table, whole("duo"))
        k5_early = placed("k5_early", W, U32, AT_DS_LAST)
        gather(k5_early[:], d_table, entries("k5", 0, W))
        k4_early = placed("k4_early", W, U32, AT_DS_LAST + 2 * S)
        gather(k4_early[:], d_table, entries("k4", 0, W))
        late_got = placed("late_got", 2 * W, U8, AT_TURNED)
        gather(late_got[:, 0:W], d_bytes, entries("k4", W, S))
        gather(late_got[:, W : 2 * W], d_bytes, entries("k5", W, S))
        place_rows(nc.sync, late_planes, 0, late_got)
        late_codes = placed("late_codes", 2 * W, U32, AT_Z)
        gather(late_codes[:, 0:W], d_table, entries("k4", W, S))
        gather(late_codes[:, W : 2 * W], d_table, entries("k5", W, S))

        k4_halves = [(k4_early[:], early_planes[:, S : S + W]), (late_codes[:, 0:W], late_planes[:, 0:W])]
        k5_halves = [(k5_early[:], early_planes[:, S + W : S + 2 * W]), (late_codes[:, W : 2 * W], late_planes[:, W : 2 * W])]
        h2_bank_numbers = (6, 7, 0, 1)
        pa2, pa2_23 = pair_tiles("pa2_")
        nb2, nb2_23 = pair_tiles("nb2_")
        ra2, ra2_23 = pair_tiles("ra2_")
        for m in range(BLOCKS):
            cols = slice((m % 2) * P, (m % 2 + 1) * P)
            h2_bank = bank("h2_bank%d" % m, h2_bank_numbers[m])
            passes = (
                (k5_halves[m // 2], duo_codes[:], early_planes[:, 0:S]),
                (k4_halves[m // 2], z_codes[:], z_plane[:]),
            )
            for a, ((codes, plane), moving, moving_plane) in enumerate(passes):
                nc.tensor.matmul_mx(
                    out=h2_bank[:],
                    lhsT=codes[:, cols].bitcast(FP8X4),
                    lhsT_scale=plane[:, cols],
                    rhs=moving.bitcast(FP8X4),
                    rhs_scale=moving_plane,
                    start=(a == 0),
                    stop=(a == 1),
                )
            fetch_pairs("h2_%d" % m, h2_bank, m, pa2[m], "n6", nb2[m], "n7", -1.0)

        result = [new("result%d" % m, S, F32) for m in range(BLOCKS)]

        def larger(dst, negated, plain):
            nc.vector.scalar_tensor_tensor(dst, negated, -1.0, plain, ALU.mult, ALU.max)

        def put_difference(m, lo=0, hi=W):
            nc.vector.tensor_tensor(result[m][:].indirect(entries("n9", lo, hi)), pa2[m][:, lo:hi], nb2[m][:, lo:hi], ALU.add)

        def put_larger_and_store(m):
            nc.vector.tensor_copy(result[m][:].indirect(whole("n8")), ra2[m])
            nc.sync.dma_start(out=out[m * P : (m + 1) * P, :], in_=result[m][:])

        put_difference(0, 0, W // 2)
        larger(ra2[0], nb2[0], pa2[0])
        put_difference(0, W // 2, W)
        put_larger_and_store(0)
        larger(ra2[1], nb2[1], pa2[1])
        put_difference(1)
        put_larger_and_store(1)
        put_difference(2)
        larger(ra2_23, nb2_23, pa2_23)
        put_difference(3)
        put_larger_and_store(2)
        put_larger_and_store(3)
